import numpy as np
import ml_dtypes


def mxq(x, axis, fmt="e4m3"):
    dtype, down = {"e4m3": (ml_dtypes.float8_e4m3fn, 7), "e5m2": (ml_dtypes.float8_e5m2, 14)}[fmt]
    v = np.moveaxis(np.asarray(x, np.float32).astype(ml_dtypes.bfloat16).astype(np.float64), axis, -1)
    blocks = v.reshape(v.shape[:-1] + (-1, 32))
    amax = np.abs(blocks).max(-1, keepdims=True)
    byte = np.maximum(np.where(amax > 0, np.frexp(amax)[1] - 1 + 127, 0) - down, 1)
    scale = np.exp2(byte - 127.0)
    codes = (blocks / scale).astype(np.float32).astype(dtype).astype(np.float64)
    return np.moveaxis((codes * scale).reshape(v.shape), -1, axis)


WIDE = False


def mx_kscale(k, group=512):
    if not WIDE:
        return np.ones(k)
    levels = np.array([18, -18])
    if group != 512:
        return np.exp2(np.random.permutation(np.resize(levels, k // group))).repeat(group)
    if k % 512:
        return np.exp2(np.random.permutation(np.resize(levels, k // 32))).repeat(32)
    a = np.empty((k // 512, 16))
    for p in range(k // 512):
        a[p, :8] = np.random.permutation(np.resize(levels, 8))
        for g in range(8):
            far = levels[np.abs(levels - a[p, g]) >= 10]
            a[p, g + 8] = far[np.random.randint(len(far))]
    return np.exp2(a.ravel()).repeat(32)


def f64(x):
    return np.asarray(x).astype(np.float64)


def sigmoid(v):
    return 1.0 / (1.0 + np.exp(-v))


G, D, M, N = 4, 128, 128, 512


def setup_inputs():
    n = np.random.standard_normal
    s_d = mx_kscale(D, 0)
    return {
        "h": (n((G, D, N)) * s_d[:, None]).astype(np.float32),
        "wf": (n((G, D, M)) / np.sqrt(D) / s_d[:, None]).astype(np.float32),
        "xf": (n((G, M, N))).astype(np.float32),
        "xc": (n((G, M, N))).astype(np.float32),
        "hp": (n((G, M, N))).astype(np.float32),
    }


def reference(h, wf, xf, xc, hp):
    wfq = mxq(f64(wf), 1, "e4m3")
    hq = mxq(f64(h), 1, "e4m3")
    zf = wfq.transpose(0, 2, 1) @ hq
    f = sigmoid(zf + f64(xf))
    y = f * np.tanh(f64(xc)) + (1.0 - f) * f64(hp)
    return y

@@ -1,0 +1,127 @@
+from contextlib import ExitStack
+
+import concourse.mybir as mybir
+
+G, D, M, N = 4, 128, 128, 512
+FLOPS = 2 * G * D * M * N
+
+F32 = mybir.dt.float32
+BF16 = mybir.dt.bfloat16
+U32 = mybir.dt.uint32
+U8 = mybir.dt.uint8
+FP8X4 = mybir.dt.float8_e4m3fn_x4
+ACT = mybir.ActivationFunctionType
+ALU = mybir.AluOpType
+
+P = 128
+PACK = 4
+ROWS = D // PACK
+H_SPLIT = 352
+
+
+def tile_rows_cell_mgu_kernel(tc, h, wf, xf, xc, hp, out):
+    nc = tc.nc
+    with ExitStack() as ctx:
+        sb = ctx.enter_context(tc.tile_pool(name="sb", bufs=1))
+        ps = ctx.enter_context(tc.psum_pool(name="ps", bufs=1))
+        ctx.enter_context(tc.manual_schedule())
+
+        h_raw = sb.tile([P, PACK, N], F32, name="h_raw")
+        w_raw = sb.tile([P, PACK, M], F32, name="w_raw")
+        h_bf = sb.tile([P, N, PACK], BF16, name="h_bf", align_bytes=64)
+        w_bf = sb.tile([P, M, PACK], BF16, name="w_bf", align_bytes=64)
+        h_codes = sb.tile([P, N], U32, name="h_codes", align_bytes=64)
+        h_scales = sb.tile([P, N], U8, name="h_scales", align_bytes=64)
+        w_codes = sb.tile([P, M], U32, name="w_codes", align_bytes=64)
+        w_scales = sb.tile([P, M], U8, name="w_scales", align_bytes=64)
+
+        def heads(pool, tag):
+            return [pool.tile([P, N], F32, name="%s%d" % (tag, g)) for g in range(G)]
+
+        xf_t, xc_t, hp_t = heads(sb, "xf"), heads(sb, "xc"), heads(sb, "hp")
+        cand, gate_in, gate = heads(sb, "cand"), heads(sb, "gate_in"), heads(sb, "gate")
+        diff, step, y = heads(sb, "diff"), heads(sb, "step"), heads(sb, "y")
+        z = heads(ps, "z")
+
+        nc.sync.dma_start(out=h_raw[:], in_=h.rearrange("g (p j) n -> (g p) j n", j=PACK))
+        nc.sync.dma_start(out=w_raw[:], in_=wf.rearrange("g (p j) m -> (g p) j m", j=PACK))
+        order = [(xc_t, xc, 0), (hp_t, hp, 0), (xf_t, xf, 0)]
+        for g in range(1, G):
+            order += [(xf_t, xf, g), (xc_t, xc, g), (hp_t, hp, g)]
+        for tiles, src, g in order:
+            nc.sync.dma_start(out=tiles[g][:], in_=src[g])
+
+        def views(dst, src, lo, hi):
+            return (
+                dst[:, lo:hi, :].rearrange("p (c i) j -> p c j i", i=4),
+                src[:, :, lo:hi].rearrange("p j (c i) -> p c j i", i=4),
+            )
+
+        o, i = views(h_bf, h_raw, 0, N // 2)
+        nc.vector.tensor_copy(out=o, in_=i)
+        o, i = views(h_bf, h_raw, N // 2, H_SPLIT)
+        nc.vector.tensor_copy(out=o, in_=i)
+        o, i = views(h_bf, h_raw, H_SPLIT, N)
+        nc.scalar.activation(out=o, in_=i, func=ACT.Copy)
+        o, i = views(w_bf, w_raw, 0, M)
+        nc.scalar.activation(out=o, in_=i, func=ACT.Copy)
+        for c in (slice(0, N // 2), slice(N // 2, N)):
+            nc.vector.quantize_mx(
+                out=h_codes[:, c].bitcast(FP8X4), scales=h_scales[:, c], in_=h_bf[:, c, :].rearrange("p n j -> p (n j)")
+            )
+        nc.vector.quantize_mx(
+            out=w_codes[:].bitcast(FP8X4), scales=w_scales[:], in_=w_bf[:].rearrange("p m j -> p (m j)")
+        )
+        for g in range(G):
+            r = slice(ROWS * g, ROWS * (g + 1))
+            nc.tensor.matmul_mx(
+                out=z[g][:],
+                lhsT=w_codes[r, :].bitcast(FP8X4),
+                lhsT_scale=w_scales[r, :],
+                rhs=h_codes[r, :].bitcast(FP8X4),
+                rhs_scale=h_scales[r, :],
+                start=True,
+                stop=True,
+            )
+
+        full = slice(0, N)
+
+        def candidate(g):
+            nc.scalar.activation(out=cand[g][:], in_=xc_t[g][:], func=ACT.Tanh)
+
+        def gate_sum(g):
+            nc.vector.tensor_tensor(out=gate_in[g][:], in0=z[g][:], in1=xf_t[g][:], op=ALU.add)
+
+        def gate_act(g):
+            nc.scalar.activation(out=gate[g][:], in_=gate_in[g][:], func=ACT.Tanh, scale=0.5)
+
+        def difference(g):
+            nc.vector.tensor_tensor(out=diff[g][:], in0=cand[g][:], in1=hp_t[g][:], op=ALU.subtract)
+
+        def scale_step(g, c=full):
+            nc.vector.scalar_tensor_tensor(
+                out=step[g][:, c], in0=gate[g][:, c], scalar=1.0, in1=diff[g][:, c], op0=ALU.add, op1=ALU.mult
+            )
+
+        def finish(g, c=full):
+            nc.vector.scalar_tensor_tensor(
+                out=y[g][:, c], in0=step[g][:, c], scalar=0.5, in1=hp_t[g][:, c], op0=ALU.mult, op1=ALU.add
+            )
+            nc.sync.dma_start(out=out[g][:, c], in_=y[g][:, c])
+
+        candidate(0)
+        difference(0)
+        gate_sum(0)
+        gate_act(0)
+        for g in range(1, G):
+            gate_sum(g)
+            candidate(g)
+            gate_act(g)
+            scale_step(g - 1)
+            difference(g)
+            finish(g - 1)
+        halves = [slice(0, N // 2), slice(N // 2, N)]
+        for c in halves:
+            scale_step(G - 1, c)
+        for c in halves:
+            finish(G - 1, c)

@@ -16,7 +16,9 @@ ALU = mybir.AluOpType
 P = 128
 PACK = 4
 ROWS = D // PACK
-H_SPLIT = 352
+Q = 4
+W = N // Q
+W_SPLIT = 96
 
 
 def tile_rows_cell_mgu_kernel(tc, h, wf, xf, xc, hp, out):
@@ -26,102 +28,135 @@ def tile_rows_cell_mgu_kernel(tc, h, wf, xf, xc, hp, out):
         ps = ctx.enter_context(tc.psum_pool(name="ps", bufs=1))
         ctx.enter_context(tc.manual_schedule())
 
-        h_raw = sb.tile([P, PACK, N], F32, name="h_raw")
+        def stages(tag, shape, dtype, **kw):
+            return [sb.tile(shape, dtype, name="%s%d" % (tag, q), **kw) for q in range(Q)]
+
         w_raw = sb.tile([P, PACK, M], F32, name="w_raw")
-        h_bf = sb.tile([P, N, PACK], BF16, name="h_bf", align_bytes=64)
         w_bf = sb.tile([P, M, PACK], BF16, name="w_bf", align_bytes=64)
-        h_codes = sb.tile([P, N], U32, name="h_codes", align_bytes=64)
-        h_scales = sb.tile([P, N], U8, name="h_scales", align_bytes=64)
         w_codes = sb.tile([P, M], U32, name="w_codes", align_bytes=64)
         w_scales = sb.tile([P, M], U8, name="w_scales", align_bytes=64)
+        h_raw = stages("h_raw", [P, PACK, W], F32)
+        h_bf = stages("h_bf", [P, W, PACK], BF16, align_bytes=64)
+        h_codes = stages("h_codes", [P, W], U32, align_bytes=64)
+        h_scales = stages("h_scales", [P, W], U8, align_bytes=64)
+        xf_t, xc_t, hp_t = (stages(t, [P, G, W], F32) for t in ("xf", "xc", "hp"))
+        cand, gate_in, gate = (stages(t, [P, G, W], F32) for t in ("cand", "gate_in", "gate"))
+        diff, step, y = (stages(t, [P, G, W], F32) for t in ("diff", "step", "y"))
+        z = [[ps.tile([P, 2 * W], F32, name="z%d_%d" % (g, b)) for b in range(2)] for g in range(G)]
 
-        def heads(pool, tag):
-            return [pool.tile([P, N], F32, name="%s%d" % (tag, g)) for g in range(G)]
+        def cols(q):
+            return slice(W * q, W * (q + 1))
 
-        xf_t, xc_t, hp_t = heads(sb, "xf"), heads(sb, "xc"), heads(sb, "hp")
-        cand, gate_in, gate = heads(sb, "cand"), heads(sb, "gate_in"), heads(sb, "gate")
-        diff, step, y = heads(sb, "diff"), heads(sb, "step"), heads(sb, "y")
-        z = heads(ps, "z")
+        def zq(g, q):
+            return z[g][q % 2][:, cols(q // 2)]
 
-        nc.sync.dma_start(out=h_raw[:], in_=h.rearrange("g (p j) n -> (g p) j n", j=PACK))
-        nc.sync.dma_start(out=w_raw[:], in_=wf.rearrange("g (p j) m -> (g p) j m", j=PACK))
-        order = [(xc_t, xc, 0), (hp_t, hp, 0), (xf_t, xf, 0)]
-        for g in range(1, G):
-            order += [(xf_t, xf, g), (xc_t, xc, g), (hp_t, hp, g)]
-        for tiles, src, g in order:
-            nc.sync.dma_start(out=tiles[g][:], in_=src[g])
+        h_v = h.rearrange("g (p j) n -> (g p) j n", j=PACK)
+        src = {
+            "h": (h_raw, h_v),
+            "xf": (xf_t, xf.rearrange("g m n -> m g n")),
+            "xc": (xc_t, xc.rearrange("g m n -> m g n")),
+            "hp": (hp_t, hp.rearrange("g m n -> m g n")),
+        }
+        out_v = out.rearrange("g m n -> m g n")
+        for name in "h0 w h1 xf0 xc0 hp0 xf1 h2 xc1 hp1 xf2 h3 xc2 hp2 xf3 xc3 hp3".split():
+            if name == "w":
+                nc.sync.dma_start(out=w_raw[:], in_=wf.rearrange("g (p j) m -> (g p) j m", j=PACK))
+            else:
+                tiles, view = src[name[:-1]]
+                q = int(name[-1])
+                nc.sync.dma_start(out=tiles[q][:], in_=view[:, :, cols(q)])
 
-        def views(dst, src, lo, hi):
+        def views(dst, raw, lo, hi):
             return (
                 dst[:, lo:hi, :].rearrange("p (c i) j -> p c j i", i=4),
-                src[:, :, lo:hi].rearrange("p j (c i) -> p c j i", i=4),
+                raw[:, :, lo:hi].rearrange("p j (c i) -> p c j i", i=4),
             )
 
-        o, i = views(h_bf, h_raw, 0, N // 2)
-        nc.vector.tensor_copy(out=o, in_=i)
-        o, i = views(h_bf, h_raw, N // 2, H_SPLIT)
-        nc.vector.tensor_copy(out=o, in_=i)
-        o, i = views(h_bf, h_raw, H_SPLIT, N)
-        nc.scalar.activation(out=o, in_=i, func=ACT.Copy)
-        o, i = views(w_bf, w_raw, 0, M)
-        nc.scalar.activation(out=o, in_=i, func=ACT.Copy)
-        for c in (slice(0, N // 2), slice(N // 2, N)):
+        def cast_vector(dst, raw, lo, hi):
+            o, i = views(dst, raw, lo, hi)
+            nc.vector.tensor_copy(out=o, in_=i)
+
+        def cast_scalar(dst, raw, lo, hi):
+            o, i = views(dst, raw, lo, hi)
+            nc.scalar.activation(out=o, in_=i, func=ACT.Copy)
+
+        def quantise(codes, scales, packed):
             nc.vector.quantize_mx(
-                out=h_codes[:, c].bitcast(FP8X4), scales=h_scales[:, c], in_=h_bf[:, c, :].rearrange("p n j -> p (n j)")
-            )
-        nc.vector.quantize_mx(
-            out=w_codes[:].bitcast(FP8X4), scales=w_scales[:], in_=w_bf[:].rearrange("p m j -> p (m j)")
-        )
-        for g in range(G):
-            r = slice(ROWS * g, ROWS * (g + 1))
-            nc.tensor.matmul_mx(
-                out=z[g][:],
-                lhsT=w_codes[r, :].bitcast(FP8X4),
-                lhsT_scale=w_scales[r, :],
-                rhs=h_codes[r, :].bitcast(FP8X4),
-                rhs_scale=h_scales[r, :],
-                start=True,
-                stop=True,
+                out=codes[:].bitcast(FP8X4), scales=scales[:], in_=packed[:].rearrange("p n j -> p (n j)")
             )
 
-        full = slice(0, N)
+        def products(q):
+            for g in range(G):
+                r = slice(ROWS * g, ROWS * (g + 1))
+                nc.tensor.matmul_mx(
+                    out=zq(g, q),
+                    lhsT=w_codes[r, :].bitcast(FP8X4),
+                    lhsT_scale=w_scales[r, :],
+                    rhs=h_codes[q][r, :].bitcast(FP8X4),
+                    rhs_scale=h_scales[q][r, :],
+                    start=True,
+                    stop=True,
+                )
 
-        def candidate(g):
-            nc.scalar.activation(out=cand[g][:], in_=xc_t[g][:], func=ACT.Tanh)
+        def state(q):
+            quantise(h_codes[q], h_scales[q], h_bf[q])
+            products(q)
 
-        def gate_sum(g):
-            nc.vector.tensor_tensor(out=gate_in[g][:], in0=z[g][:], in1=xf_t[g][:], op=ALU.add)
+        full = slice(0, G)
 
-        def gate_act(g):
-            nc.scalar.activation(out=gate[g][:], in_=gate_in[g][:], func=ACT.Tanh, scale=0.5)
+        def candidate(q):
+            nc.scalar.activation(out=cand[q][:], in_=xc_t[q][:], func=ACT.Tanh)
 
-        def difference(g):
-            nc.vector.tensor_tensor(out=diff[g][:], in0=cand[g][:], in1=hp_t[g][:], op=ALU.subtract)
+        def gate_sum(q):
+            for g in range(G):
+                nc.vector.tensor_tensor(out=gate_in[q][:, g, :], in0=zq(g, q), in1=xf_t[q][:, g, :], op=ALU.add)
 
-        def scale_step(g, c=full):
+        def gate_act(q):
+            nc.scalar.activation(out=gate[q][:], in_=gate_in[q][:], func=ACT.Tanh, scale=0.5)
+
+        def difference(q):
+            nc.vector.tensor_tensor(out=diff[q][:], in0=cand[q][:], in1=hp_t[q][:], op=ALU.subtract)
+
+        def scale_step(q, c=full):
             nc.vector.scalar_tensor_tensor(
-                out=step[g][:, c], in0=gate[g][:, c], scalar=1.0, in1=diff[g][:, c], op0=ALU.add, op1=ALU.mult
+                out=step[q][:, c, :], in0=gate[q][:, c, :], scalar=1.0, in1=diff[q][:, c, :], op0=ALU.add, op1=ALU.mult
             )
 
-        def finish(g, c=full):
+        def finish(q, c=full):
             nc.vector.scalar_tensor_tensor(
-                out=y[g][:, c], in0=step[g][:, c], scalar=0.5, in1=hp_t[g][:, c], op0=ALU.mult, op1=ALU.add
+                out=y[q][:, c, :], in0=step[q][:, c, :], scalar=0.5, in1=hp_t[q][:, c, :], op0=ALU.mult, op1=ALU.add
             )
-            nc.sync.dma_start(out=out[g][:, c], in_=y[g][:, c])
+            nc.sync.dma_start(out=out_v[:, c, cols(q)], in_=y[q][:, c, :])
 
-        candidate(0)
-        difference(0)
+        cast_vector(h_bf[0], h_raw[0], 0, W)
+        cast_vector(w_bf, w_raw, 0, W_SPLIT)
+        cast_scalar(w_bf, w_raw, W_SPLIT, M)
+        quantise(h_codes[0], h_scales[0], h_bf[0])
+        quantise(w_codes, w_scales, w_bf)
+        products(0)
+        cast_scalar(h_bf[1], h_raw[1], 0, W)
+        state(1)
         gate_sum(0)
+        candidate(0)
         gate_act(0)
-        for g in range(1, G):
-            gate_sum(g)
-            candidate(g)
-            gate_act(g)
-            scale_step(g - 1)
-            difference(g)
-            finish(g - 1)
-        halves = [slice(0, N // 2), slice(N // 2, N)]
+        difference(0)
+        for q in range(1, Q):
+            gate_sum(q)
+            scale_step(q - 1)
+            if q + 1 < Q:
+                cast_scalar(h_bf[q + 1], h_raw[q + 1], 0, W)
+                state(q + 1)
+                finish(q - 1)
+                candidate(q)
+                gate_act(q)
+                difference(q)
+            else:
+                candidate(q)
+                gate_act(q)
+                difference(q)
+                finish(q - 1)
+        halves = [slice(0, G // 2), slice(G // 2, G)]
         for c in halves:
-            scale_step(G - 1, c)
+            scale_step(Q - 1, c)
         for c in halves:
-            finish(G - 1, c)
+            finish(Q - 1, c)

@@ -18,7 +18,7 @@ PACK = 4
 ROWS = D // PACK
 Q = 4
 W = N // Q
-W_SPLIT = 96
+CUT = 224
 
 
 def tile_rows_cell_mgu_kernel(tc, h, wf, xf, xc, hp, out):
@@ -28,135 +28,124 @@ def tile_rows_cell_mgu_kernel(tc, h, wf, xf, xc, hp, out):
         ps = ctx.enter_context(tc.psum_pool(name="ps", bufs=1))
         ctx.enter_context(tc.manual_schedule())
 
-        def stages(tag, shape, dtype, **kw):
-            return [sb.tile(shape, dtype, name="%s%d" % (tag, q), **kw) for q in range(Q)]
+        def heads(tag):
+            return [sb.tile([P, N], F32, name="%s%d" % (tag, g)) for g in range(G)]
 
+        warm_in = sb.tile([P, 8], F32, name="warm_in")
+        warm_out = sb.tile([P, 8], F32, name="warm_out")
         w_raw = sb.tile([P, PACK, M], F32, name="w_raw")
         w_bf = sb.tile([P, M, PACK], BF16, name="w_bf", align_bytes=64)
         w_codes = sb.tile([P, M], U32, name="w_codes", align_bytes=64)
         w_scales = sb.tile([P, M], U8, name="w_scales", align_bytes=64)
-        h_raw = stages("h_raw", [P, PACK, W], F32)
-        h_bf = stages("h_bf", [P, W, PACK], BF16, align_bytes=64)
-        h_codes = stages("h_codes", [P, W], U32, align_bytes=64)
-        h_scales = stages("h_scales", [P, W], U8, align_bytes=64)
-        xf_t, xc_t, hp_t = (stages(t, [P, G, W], F32) for t in ("xf", "xc", "hp"))
-        cand, gate_in, gate = (stages(t, [P, G, W], F32) for t in ("cand", "gate_in", "gate"))
-        diff, step, y = (stages(t, [P, G, W], F32) for t in ("diff", "step", "y"))
-        z = [[ps.tile([P, 2 * W], F32, name="z%d_%d" % (g, b)) for b in range(2)] for g in range(G)]
+        h_raw = [sb.tile([P, 2, N], F32, name="h_raw%d" % u) for u in range(2)]
+        h_bf = sb.tile([P, N, PACK], BF16, name="h_bf", align_bytes=64)
+        h_codes = sb.tile([P, N], U32, name="h_codes", align_bytes=64)
+        h_scales = sb.tile([P, N], U8, name="h_scales", align_bytes=64)
+        xf_t, xc_t, hp_t = heads("xf"), heads("xc"), heads("hp")
+        cand, gate_in, gate = heads("cand"), heads("gate_in"), heads("gate")
+        diff, step, y = heads("diff"), heads("step"), heads("y")
+        z0 = [ps.tile([P, N // 2], F32, name="z0_%d" % u) for u in range(2)]
+        z = [None] + [ps.tile([P, N], F32, name="z%d" % g) for g in range(1, G)]
 
-        def cols(q):
+        full = slice(0, N)
+        lo, hi = slice(0, N // 2), slice(N // 2, N)
+        ca, cb = slice(0, CUT), slice(CUT, N)
+
+        def quarter(q):
             return slice(W * q, W * (q + 1))
 
-        def zq(g, q):
-            return z[g][q % 2][:, cols(q // 2)]
+        nc.gpsimd.memset(warm_in[:], 0.0)
+        nc.scalar.activation(out=warm_out[:], in_=warm_in[:], func=ACT.Sigmoid)
 
         h_v = h.rearrange("g (p j) n -> (g p) j n", j=PACK)
-        src = {
-            "h": (h_raw, h_v),
-            "xf": (xf_t, xf.rearrange("g m n -> m g n")),
-            "xc": (xc_t, xc.rearrange("g m n -> m g n")),
-            "hp": (hp_t, hp.rearrange("g m n -> m g n")),
-        }
-        out_v = out.rearrange("g m n -> m g n")
-        for name in "h0 w h1 xf0 xc0 hp0 xf1 h2 xc1 hp1 xf2 h3 xc2 hp2 xf3 xc3 hp3".split():
-            if name == "w":
-                nc.sync.dma_start(out=w_raw[:], in_=wf.rearrange("g (p j) m -> (g p) j m", j=PACK))
-            else:
-                tiles, view = src[name[:-1]]
-                q = int(name[-1])
-                nc.sync.dma_start(out=tiles[q][:], in_=view[:, :, cols(q)])
-
-        def views(dst, raw, lo, hi):
-            return (
-                dst[:, lo:hi, :].rearrange("p (c i) j -> p c j i", i=4),
-                raw[:, :, lo:hi].rearrange("p j (c i) -> p c j i", i=4),
-            )
-
-        def cast_vector(dst, raw, lo, hi):
-            o, i = views(dst, raw, lo, hi)
-            nc.vector.tensor_copy(out=o, in_=i)
-
-        def cast_scalar(dst, raw, lo, hi):
-            o, i = views(dst, raw, lo, hi)
-            nc.scalar.activation(out=o, in_=i, func=ACT.Copy)
+        nc.sync.dma_start(out=w_raw[:], in_=wf.rearrange("g (p j) m -> (g p) j m", j=PACK))
+        for u in range(2):
+            nc.sync.dma_start(out=h_raw[u][:], in_=h_v[:, 2 * u : 2 * u + 2, :])
+        src = {"xf": (xf_t, xf), "xc": (xc_t, xc), "hp": (hp_t, hp)}
+        for name in "xc0 xf0 hp0 xf1 xc1 hp1 xf2 xc2 hp2 xc3 hp3 xf3".split():
+            tiles, view = src[name[:-1]]
+            g = int(name[-1])
+            nc.sync.dma_start(out=tiles[g][:], in_=view[g])
 
         def quantise(codes, scales, packed):
-            nc.vector.quantize_mx(
-                out=codes[:].bitcast(FP8X4), scales=scales[:], in_=packed[:].rearrange("p n j -> p (n j)")
-            )
+            nc.vector.quantize_mx(out=codes.bitcast(FP8X4), scales=scales, in_=packed.rearrange("p n j -> p (n j)"))
 
-        def products(q):
-            for g in range(G):
-                r = slice(ROWS * g, ROWS * (g + 1))
+        nc.vector.tensor_copy(
+            out=w_bf[:].rearrange("p (c i) j -> p c j i", i=4), in_=w_raw[:].rearrange("p j (c i) -> p c j i", i=4)
+        )
+        quantise(w_codes[:], w_scales[:], w_bf[:])
+        nc.vector.tensor_copy(out=h_bf[:, :, 0:2], in_=h_raw[0][:].rearrange("p j n -> p n j"))
+        for q in range(Q):
+            o, i = h_bf[:, quarter(q), 2:4], h_raw[1][:, :, quarter(q)].rearrange("p j n -> p n j")
+            if q < 2:
+                nc.vector.tensor_copy(out=o, in_=i)
+            else:
+                nc.scalar.activation(out=o, in_=i, func=ACT.Copy)
+        for q in range(Q):
+            quantise(h_codes[:, quarter(q)], h_scales[:, quarter(q)], h_bf[:, quarter(q), :])
+        for g in range(G):
+            r = slice(ROWS * g, ROWS * (g + 1))
+            for q in range(Q):
                 nc.tensor.matmul_mx(
-                    out=zq(g, q),
+                    out=z0[q // 2][:, quarter(q % 2)] if g == 0 else z[g][:, quarter(q)],
                     lhsT=w_codes[r, :].bitcast(FP8X4),
                     lhsT_scale=w_scales[r, :],
-                    rhs=h_codes[q][r, :].bitcast(FP8X4),
-                    rhs_scale=h_scales[q][r, :],
+                    rhs=h_codes[r, quarter(q)].bitcast(FP8X4),
+                    rhs_scale=h_scales[r, quarter(q)],
                     start=True,
                     stop=True,
                 )
 
-        def state(q):
-            quantise(h_codes[q], h_scales[q], h_bf[q])
-            products(q)
+        def candidate(g, c=full):
+            nc.scalar.activation(out=cand[g][:, c], in_=xc_t[g][:, c], func=ACT.Tanh)
 
-        full = slice(0, G)
+        def gate_sum(g, c, zz):
+            nc.vector.tensor_tensor(out=gate_in[g][:, c], in0=zz, in1=xf_t[g][:, c], op=ALU.add)
 
-        def candidate(q):
-            nc.scalar.activation(out=cand[q][:], in_=xc_t[q][:], func=ACT.Tanh)
+        def gate_act(g, c=full):
+            nc.scalar.activation(out=gate[g][:, c], in_=gate_in[g][:, c], func=ACT.Sigmoid)
 
-        def gate_sum(q):
-            for g in range(G):
-                nc.vector.tensor_tensor(out=gate_in[q][:, g, :], in0=zq(g, q), in1=xf_t[q][:, g, :], op=ALU.add)
+        def difference(eng, g, c=full):
+            eng.tensor_tensor(out=diff[g][:, c], in0=cand[g][:, c], in1=hp_t[g][:, c], op=ALU.subtract)
 
-        def gate_act(q):
-            nc.scalar.activation(out=gate[q][:], in_=gate_in[q][:], func=ACT.Tanh, scale=0.5)
+        def scale_step(eng, g, c=full):
+            eng.tensor_tensor(out=step[g][:, c], in0=gate[g][:, c], in1=diff[g][:, c], op=ALU.mult)
 
-        def difference(q):
-            nc.vector.tensor_tensor(out=diff[q][:], in0=cand[q][:], in1=hp_t[q][:], op=ALU.subtract)
+        def finish(eng, g, c=full):
+            eng.tensor_tensor(out=y[g][:, c], in0=step[g][:, c], in1=hp_t[g][:, c], op=ALU.add)
 
-        def scale_step(q, c=full):
-            nc.vector.scalar_tensor_tensor(
-                out=step[q][:, c, :], in0=gate[q][:, c, :], scalar=1.0, in1=diff[q][:, c, :], op0=ALU.add, op1=ALU.mult
-            )
+        def store(g, c=full):
+            nc.sync.dma_start(out=out[g][:, c], in_=y[g][:, c])
 
-        def finish(q, c=full):
-            nc.vector.scalar_tensor_tensor(
-                out=y[q][:, c, :], in0=step[q][:, c, :], scalar=0.5, in1=hp_t[q][:, c, :], op0=ALU.mult, op1=ALU.add
-            )
-            nc.sync.dma_start(out=out_v[:, c, cols(q)], in_=y[q][:, c, :])
-
-        cast_vector(h_bf[0], h_raw[0], 0, W)
-        cast_vector(w_bf, w_raw, 0, W_SPLIT)
-        cast_scalar(w_bf, w_raw, W_SPLIT, M)
-        quantise(h_codes[0], h_scales[0], h_bf[0])
-        quantise(w_codes, w_scales, w_bf)
-        products(0)
-        cast_scalar(h_bf[1], h_raw[1], 0, W)
-        state(1)
-        gate_sum(0)
+        V, GP = nc.vector, nc.gpsimd
         candidate(0)
-        gate_act(0)
-        difference(0)
-        for q in range(1, Q):
-            gate_sum(q)
-            scale_step(q - 1)
-            if q + 1 < Q:
-                cast_scalar(h_bf[q + 1], h_raw[q + 1], 0, W)
-                state(q + 1)
-                finish(q - 1)
-                candidate(q)
-                gate_act(q)
-                difference(q)
-            else:
-                candidate(q)
-                gate_act(q)
-                difference(q)
-                finish(q - 1)
-        halves = [slice(0, G // 2), slice(G // 2, G)]
-        for c in halves:
-            scale_step(Q - 1, c)
-        for c in halves:
-            finish(Q - 1, c)
+        gate_sum(0, lo, z0[0][:])
+        gate_act(0, lo)
+        difference(GP, 0, ca)
+        gate_sum(0, hi, z0[1][:])
+        gate_act(0, hi)
+        difference(V, 0, cb)
+        scale_step(GP, 0, ca)
+        gate_sum(1, full, z[1][:])
+        candidate(1)
+        gate_act(1)
+        scale_step(V, 0, cb)
+        difference(V, 1)
+        finish(V, 0)
+        store(0)
+        for g in range(1, G - 1):
+            scale_step(V, g, ca)
+            scale_step(V, g, cb)
+            finish(GP, g, ca)
+            candidate(g + 1)
+            gate_sum(g + 1, full, z[g + 1][:])
+            gate_act(g + 1, lo)
+            gate_act(g + 1, hi)
+            difference(V, g + 1)
+            finish(V, g, cb)
+            store(g)
+        for c in (lo, hi):
+            scale_step(V, G - 1, c)
+        for c in (lo, hi):
+            finish(V, G - 1, c)
+            store(G - 1, c)

@@ -18,7 +18,7 @@ PACK = 4
 ROWS = D // PACK
 Q = 4
 W = N // Q
-CUT = 224
+CUT = 384
 
 
 def tile_rows_cell_mgu_kernel(tc, h, wf, xf, xc, hp, out):
@@ -62,7 +62,7 @@ def tile_rows_cell_mgu_kernel(tc, h, wf, xf, xc, hp, out):
         for u in range(2):
             nc.sync.dma_start(out=h_raw[u][:], in_=h_v[:, 2 * u : 2 * u + 2, :])
         src = {"xf": (xf_t, xf), "xc": (xc_t, xc), "hp": (hp_t, hp)}
-        for name in "xc0 xf0 hp0 xf1 xc1 hp1 xf2 xc2 hp2 xc3 hp3 xf3".split():
+        for name in "xc0 hp0 xf0 xf1 xc1 hp1 xf2 xf3 xc2 hp2 xc3 hp3".split():
             tiles, view = src[name[:-1]]
             g = int(name[-1])
             nc.sync.dma_start(out=tiles[g][:], in_=view[g])
@@ -118,34 +118,41 @@ def tile_rows_cell_mgu_kernel(tc, h, wf, xf, xc, hp, out):
             nc.sync.dma_start(out=out[g][:, c], in_=y[g][:, c])
 
         V, GP = nc.vector, nc.gpsimd
-        candidate(0)
+        candidate(0, lo)
+        candidate(0, hi)
+        difference(V, 0, lo)
+        difference(GP, 0, hi)
         gate_sum(0, lo, z0[0][:])
         gate_act(0, lo)
-        difference(GP, 0, ca)
         gate_sum(0, hi, z0[1][:])
         gate_act(0, hi)
-        difference(V, 0, cb)
-        scale_step(GP, 0, ca)
         gate_sum(1, full, z[1][:])
         candidate(1)
         gate_act(1)
-        scale_step(V, 0, cb)
+        scale_step(V, 0, lo)
+        scale_step(V, 0, hi)
+        finish(V, 0, lo)
         difference(V, 1)
-        finish(V, 0)
+        finish(V, 0, hi)
         store(0)
-        for g in range(1, G - 1):
-            scale_step(V, g, ca)
-            scale_step(V, g, cb)
-            finish(GP, g, ca)
-            candidate(g + 1)
-            gate_sum(g + 1, full, z[g + 1][:])
-            gate_act(g + 1, lo)
-            gate_act(g + 1, hi)
-            difference(V, g + 1)
-            finish(V, g, cb)
-            store(g)
+        scale_step(V, 1, ca)
+        scale_step(V, 1, cb)
+        finish(GP, 1, ca)
+        gate_sum(2, full, z[2][:])
+        gate_sum(3, full, z[3][:])
+        candidate(2)
+        gate_act(2)
+        candidate(3)
+        gate_act(3)
+        difference(V, 2)
+        finish(V, 1, cb)
+        store(1)
+        scale_step(V, 2)
+        difference(V, 3)
+        finish(V, 2)
+        store(2)
         for c in (lo, hi):
-            scale_step(V, G - 1, c)
+            scale_step(V, 3, c)
         for c in (lo, hi):
-            finish(V, G - 1, c)
-            store(G - 1, c)
+            finish(V, 3, c)
+            store(3, c)

@@ -74,7 +74,10 @@ def tile_rows_cell_mgu_kernel(tc, h, wf, xf, xc, hp, out):
             out=w_bf[:].rearrange("p (c i) j -> p c j i", i=4), in_=w_raw[:].rearrange("p j (c i) -> p c j i", i=4)
         )
         quantise(w_codes[:], w_scales[:], w_bf[:])
-        nc.vector.tensor_copy(out=h_bf[:, :, 0:2], in_=h_raw[0][:].rearrange("p j n -> p n j"))
+        nc.vector.tensor_copy(out=h_bf[:, 0:320, 0:2], in_=h_raw[0][:, :, 0:320].rearrange("p j n -> p n j"))
+        nc.scalar.activation(
+            out=h_bf[:, 320:N, 0:2], in_=h_raw[0][:, :, 320:N].rearrange("p j n -> p n j"), func=ACT.Copy
+        )
         for q in range(Q):
             o, i = h_bf[:, quarter(q), 2:4], h_raw[1][:, :, quarter(q)].rearrange("p j n -> p n j")
             if q < 2:
@@ -83,9 +86,11 @@ def tile_rows_cell_mgu_kernel(tc, h, wf, xf, xc, hp, out):
                 nc.scalar.activation(out=o, in_=i, func=ACT.Copy)
         for q in range(Q):
             quantise(h_codes[:, quarter(q)], h_scales[:, quarter(q)], h_bf[:, quarter(q), :])
-        for g in range(G):
+        order = [(0, 0), (0, 1), (1, 0), (0, 2), (1, 1), (0, 3), (1, 2), (1, 3)]
+        order += [(g, q) for q in range(Q) for g in (2, 3)]
+        for g, q in order:
             r = slice(ROWS * g, ROWS * (g + 1))
-            for q in range(Q):
+            if True:
                 nc.tensor.matmul_mx(
                     out=z0[q // 2][:, quarter(q % 2)] if g == 0 else z[g][:, quarter(q)],
                     lhsT=w_codes[r, :].bitcast(FP8X4),

from contextlib import ExitStack

import concourse.mybir as mybir

G, D, M, N = 4, 128, 128, 512
FLOPS = 2 * G * D * M * N

F32 = mybir.dt.float32
BF16 = mybir.dt.bfloat16
U32 = mybir.dt.uint32
U8 = mybir.dt.uint8
FP8X4 = mybir.dt.float8_e4m3fn_x4
ACT = mybir.ActivationFunctionType
ALU = mybir.AluOpType

P = 128
PACK = 4
ROWS = D // PACK
Q = 4
W = N // Q
CUT = 384


def tile_rows_cell_mgu_kernel(tc, h, wf, xf, xc, hp, out):
    nc = tc.nc
    with ExitStack() as ctx:
        sb = ctx.enter_context(tc.tile_pool(name="sb", bufs=1))
        ps = ctx.enter_context(tc.psum_pool(name="ps", bufs=1))
        ctx.enter_context(tc.manual_schedule())

        def heads(tag):
            return [sb.tile([P, N], F32, name="%s%d" % (tag, g)) for g in range(G)]

        warm_in = sb.tile([P, 8], F32, name="warm_in")
        warm_out = sb.tile([P, 8], F32, name="warm_out")
        w_raw = sb.tile([P, PACK, M], F32, name="w_raw")
        w_bf = sb.tile([P, M, PACK], BF16, name="w_bf", align_bytes=64)
        w_codes = sb.tile([P, M], U32, name="w_codes", align_bytes=64)
        w_scales = sb.tile([P, M], U8, name="w_scales", align_bytes=64)
        h_raw = [sb.tile([P, 2, N], F32, name="h_raw%d" % u) for u in range(2)]
        h_bf = sb.tile([P, N, PACK], BF16, name="h_bf", align_bytes=64)
        h_codes = sb.tile([P, N], U32, name="h_codes", align_bytes=64)
        h_scales = sb.tile([P, N], U8, name="h_scales", align_bytes=64)
        xf_t, xc_t, hp_t = heads("xf"), heads("xc"), heads("hp")
        cand, gate_in, gate = heads("cand"), heads("gate_in"), heads("gate")
        diff, step, y = heads("diff"), heads("step"), heads("y")
        z0 = [ps.tile([P, N // 2], F32, name="z0_%d" % u) for u in range(2)]
        z = [None] + [ps.tile([P, N], F32, name="z%d" % g) for g in range(1, G)]

        full = slice(0, N)
        lo, hi = slice(0, N // 2), slice(N // 2, N)
        ca, cb = slice(0, CUT), slice(CUT, N)

        def quarter(q):
            return slice(W * q, W * (q + 1))

        nc.gpsimd.memset(warm_in[:], 0.0)
        nc.scalar.activation(out=warm_out[:], in_=warm_in[:], func=ACT.Sigmoid)

        h_v = h.rearrange("g (p j) n -> (g p) j n", j=PACK)
        nc.sync.dma_start(out=w_raw[:], in_=wf.rearrange("g (p j) m -> (g p) j m", j=PACK))
        for u in range(2):
            nc.sync.dma_start(out=h_raw[u][:], in_=h_v[:, 2 * u : 2 * u + 2, :])
        src = {"xf": (xf_t, xf), "xc": (xc_t, xc), "hp": (hp_t, hp)}
        for name in "xc0 hp0 xf0 xf1 xc1 hp1 xf2 xf3 xc2 hp2 xc3 hp3".split():
            tiles, view = src[name[:-1]]
            g = int(name[-1])
            nc.sync.dma_start(out=tiles[g][:], in_=view[g])

        def quantise(codes, scales, packed):
            nc.vector.quantize_mx(out=codes.bitcast(FP8X4), scales=scales, in_=packed.rearrange("p n j -> p (n j)"))

        nc.vector.tensor_copy(
            out=w_bf[:].rearrange("p (c i) j -> p c j i", i=4), in_=w_raw[:].rearrange("p j (c i) -> p c j i", i=4)
        )
        quantise(w_codes[:], w_scales[:], w_bf[:])
        nc.vector.tensor_copy(out=h_bf[:, 0:320, 0:2], in_=h_raw[0][:, :, 0:320].rearrange("p j n -> p n j"))
        nc.scalar.activation(
            out=h_bf[:, 320:N, 0:2], in_=h_raw[0][:, :, 320:N].rearrange("p j n -> p n j"), func=ACT.Copy
        )
        for q in range(Q):
            o, i = h_bf[:, quarter(q), 2:4], h_raw[1][:, :, quarter(q)].rearrange("p j n -> p n j")
            if q < 2:
                nc.vector.tensor_copy(out=o, in_=i)
            else:
                nc.scalar.activation(out=o, in_=i, func=ACT.Copy)
        for q in range(Q):
            quantise(h_codes[:, quarter(q)], h_scales[:, quarter(q)], h_bf[:, quarter(q), :])
        order = [(0, 0), (0, 1), (1, 0), (0, 2), (1, 1), (0, 3), (1, 2), (1, 3)]
        order += [(g, q) for q in range(Q) for g in (2, 3)]
        for g, q in order:
            r = slice(ROWS * g, ROWS * (g + 1))
            if True:
                nc.tensor.matmul_mx(
                    out=z0[q // 2][:, quarter(q % 2)] if g == 0 else z[g][:, quarter(q)],
                    lhsT=w_codes[r, :].bitcast(FP8X4),
                    lhsT_scale=w_scales[r, :],
                    rhs=h_codes[r, quarter(q)].bitcast(FP8X4),
                    rhs_scale=h_scales[r, quarter(q)],
                    start=True,
                    stop=True,
                )

        def candidate(g, c=full):
            nc.scalar.activation(out=cand[g][:, c], in_=xc_t[g][:, c], func=ACT.Tanh)

        def gate_sum(g, c, zz):
            nc.vector.tensor_tensor(out=gate_in[g][:, c], in0=zz, in1=xf_t[g][:, c], op=ALU.add)

        def gate_act(g, c=full):
            nc.scalar.activation(out=gate[g][:, c], in_=gate_in[g][:, c], func=ACT.Sigmoid)

        def difference(eng, g, c=full):
            eng.tensor_tensor(out=diff[g][:, c], in0=cand[g][:, c], in1=hp_t[g][:, c], op=ALU.subtract)

        def scale_step(eng, g, c=full):
            eng.tensor_tensor(out=step[g][:, c], in0=gate[g][:, c], in1=diff[g][:, c], op=ALU.mult)

        def finish(eng, g, c=full):
            eng.tensor_tensor(out=y[g][:, c], in0=step[g][:, c], in1=hp_t[g][:, c], op=ALU.add)

        def store(g, c=full):
            nc.sync.dma_start(out=out[g][:, c], in_=y[g][:, c])

        V, GP = nc.vector, nc.gpsimd
        candidate(0, lo)
        candidate(0, hi)
        difference(V, 0, lo)
        difference(GP, 0, hi)
        gate_sum(0, lo, z0[0][:])
        gate_act(0, lo)
        gate_sum(0, hi, z0[1][:])
        gate_act(0, hi)
        gate_sum(1, full, z[1][:])
        candidate(1)
        gate_act(1)
        scale_step(V, 0, lo)
        scale_step(V, 0, hi)
        finish(V, 0, lo)
        difference(V, 1)
        finish(V, 0, hi)
        store(0)
        scale_step(V, 1, ca)
        scale_step(V, 1, cb)
        finish(GP, 1, ca)
        gate_sum(2, full, z[2][:])
        gate_sum(3, full, z[3][:])
        candidate(2)
        gate_act(2)
        candidate(3)
        gate_act(3)
        difference(V, 2)
        finish(V, 1, cb)
        store(1)
        scale_step(V, 2)
        difference(V, 3)
        finish(V, 2)
        store(2)
        for c in (lo, hi):
            scale_step(V, 3, c)
        for c in (lo, hi):
            finish(V, 3, c)
            store(3, c)
